import numpy as np
CORES = [2,18,34,50,66,82,98,114]
N = 8
ROOT = 3
def setup_inputs(rng):
    return {"x": rng.standard_normal((N, 128, 512), dtype=np.float32)}
def reference(x):
    y = np.full((N, 128, N * 512), np.nan, x.dtype)
    y[ROOT] = np.concatenate(list(x), axis=1)
    return {"y": y}

@@ -1,0 +1,79 @@
+K = 4
+UW = 512 // K
+LAT = 3.0
+ASSIGN = {0: 'AAAA', 1: 'AAAA', 2: 'BBBB', 4: 'CBBB', 5: 'CCCC', 6: 'DDCC', 7: 'DDDD'}
+COPIES = [(0, 1), (2, 2), (4, 5), (6, 7)]
+SCRATCH = {'land': ('sbuf', [128, 4096], 'float32')}
+SEMAPHORES = ['ld', 'sent', 'stored'] + ['a%d' % i for i in range(32)]
+
+def plan(cores, root_rank):
+    root = cores[root_rank]
+    mate = root // 8 ^ 1
+    hops = {}
+    est = {}
+    for p in 'ABCD':
+        lists = [[(j, q) for q in range(K) if ASSIGN[j][q] == p] for j in sorted(ASSIGN)]
+        lists = [x for x in lists if x]
+        lists.sort(key=lambda x: (x[0][1], -len(x)))
+        stream = []
+        i = 0
+        while any((i < len(x) for x in lists)):
+            stream += [x[i] for x in lists if i < len(x)]
+            i += 1
+        for pos, (j, q) in enumerate(stream):
+            src = cores[j]
+            base = src // 8 * 8
+            alt = pos % 2
+            if p == 'A':
+                h = [src, root]
+            elif p == 'B':
+                h = [src, base + 4 + alt, root]
+            elif p == 'C':
+                h = [src, mate * 8 + 2 + alt, root]
+            else:
+                h = [src, base + 6 + alt, mate * 8 + 6 + alt, root]
+            hops[j, q] = h
+            est[j, q] = LAT * (len(h) - 1) + pos + 1
+    return (hops, est)
+
+def rank_program(g, core, T, topo):
+    s = T.sem
+    arr = [s.a0, s.a1, s.a2, s.a3, s.a4, s.a5, s.a6, s.a7, s.a8, s.a9, s.a10, s.a11, s.a12, s.a13, s.a14, s.a15, s.a16, s.a17, s.a18, s.a19, s.a20, s.a21, s.a22, s.a23, s.a24, s.a25, s.a26, s.a27, s.a28, s.a29, s.a30, s.a31]
+    cores = list(T.cores)
+    root_rank = T.root if T.root is not None else 3
+    root = cores[root_rank]
+    hops, est = plan(cores, root_rank)
+    rank = T.rank_of(core)
+
+    def engines(a, b):
+        m = topo.mask(a, b)
+        return (m, bin(m).count('1'))
+    if core == root:
+        g.dma_start(T.y[:, 512 * root_rank:512 * (root_rank + 1)], T.x[:, :]).then_inc(s.stored, 16)
+        n = 1
+        for j0, j1 in COPIES:
+            for j in range(j0, j1 + 1):
+                for q in range(K):
+                    g.wait_ge(arr[j * K + q], engines(hops[j, q][-2], root)[1])
+            g.dma_start(T.y[:, 512 * j0:512 * (j1 + 1)], T.land[:, 512 * j0:512 * (j1 + 1)]).then_inc(s.stored, 16)
+            n += 1
+        g.wait_ge(s.stored, 16 * n)
+        return
+    work = sorted(((est[u] - LAT * (len(h) - 1 - h.index(core)), u, h.index(core)) for u, h in hops.items() if core in h[:-1]))
+    if not work:
+        return
+    if rank is not None:
+        work.sort(key=lambda w: w[1][1])
+        g.dma_start(T.land[:, 512 * rank:512 * (rank + 1)], T.x[:, :]).then_inc(s.ld, 16)
+        g.wait_ge(s.ld, 16)
+    sent = 0
+    for t, (j, q), k in work:
+        h = hops[j, q]
+        if k > 0:
+            g.wait_ge(arr[j * K + q], engines(h[k - 1], core)[1])
+        m, ne = engines(core, h[k + 1])
+        rid, pid, se = topo.addr(h[k + 1])
+        ap = T.land[:, 512 * j + UW * q:512 * j + UW * (q + 1)]
+        g.remote_dma(ap, ap, arr[j * K + q], s.sent, pid, rid, m)
+        sent += ne
+    g.wait_ge(s.sent, sent)

@@ -1,10 +1,16 @@
+MODE = 'dram'
 K = 4
 UW = 512 // K
+UR = 128 // K
 LAT = 3.0
+SMAX = 2
 ASSIGN = {0: 'AAAA', 1: 'AAAA', 2: 'BBBB', 4: 'CBBB', 5: 'CCCC', 6: 'DDCC', 7: 'DDDD'}
-COPIES = [(0, 1), (2, 2), (4, 5), (6, 7)]
-SCRATCH = {'land': ('sbuf', [128, 4096], 'float32')}
-SEMAPHORES = ['ld', 'sent', 'stored'] + ['a%d' % i for i in range(32)]
+if MODE == 'dram':
+    SCRATCH = {'land': ('dram', [8 * K, 128, UW], 'float32')}
+else:
+    SCRATCH = {'land': ('sbuf', [128, 4096], 'float32')}
+SEMAPHORES = ['sent', 'st', 'stg'] + ['ld%d' % i for i in range(4)] + ['a%d' % i for i in range(32)]
+
 
 def plan(cores, root_rank):
     root = cores[root_rank]
@@ -27,53 +33,86 @@ def plan(cores, root_rank):
             if p == 'A':
                 h = [src, root]
             elif p == 'B':
-                h = [src, base + 4 + alt, root]
+                free = [4, 5] if 'D' in ASSIGN[j] else [4, 5, 6, 7]
+                h = [src, base + free[q % len(free)], root]
             elif p == 'C':
                 h = [src, mate * 8 + 2 + alt, root]
             else:
-                h = [src, base + 6 + alt, mate * 8 + 6 + alt, root]
+                h = [src, base + 6 + q % 2, mate * 8 + 6 + alt, root]
             hops[j, q] = h
             est[j, q] = LAT * (len(h) - 1) + pos + 1
     return (hops, est)
 
+
 def rank_program(g, core, T, topo):
     s = T.sem
     arr = [s.a0, s.a1, s.a2, s.a3, s.a4, s.a5, s.a6, s.a7, s.a8, s.a9, s.a10, s.a11, s.a12, s.a13, s.a14, s.a15, s.a16, s.a17, s.a18, s.a19, s.a20, s.a21, s.a22, s.a23, s.a24, s.a25, s.a26, s.a27, s.a28, s.a29, s.a30, s.a31]
+    ld = [s.ld0, s.ld1, s.ld2, s.ld3]
     cores = list(T.cores)
     root_rank = T.root if T.root is not None else 3
     root = cores[root_rank]
     hops, est = plan(cores, root_rank)
     rank = T.rank_of(core)
 
-    def engines(a, b):
-        m = topo.mask(a, b)
-        return (m, bin(m).count('1'))
+    def ne(a, b):
+        return bin(topo.mask(a, b)).count('1')
+
+    def unit(j, q):
+        if MODE == 'dram':
+            return T.land[j * K + q]
+        return T.land[:, 512 * j + UW * q:512 * j + UW * (q + 1)]
+
+    def block(j, q0, q1):
+        if MODE == 'dram':
+            return T.land[j * K + q0:j * K + q1]
+        return T.land[:, 512 * j + UW * q0:512 * j + UW * q1]
+
+    def xblock(q0, q1):
+        if MODE == 'dram':
+            return T.x[UR * q0:UR * q1, :]
+        return T.x[:, UW * q0:UW * q1]
+
+    def yblock(j, q0, q1):
+        if MODE == 'dram':
+            return T.y[UR * q0:UR * q1, 512 * j:512 * (j + 1)]
+        return T.y[:, 512 * j + UW * q0:512 * j + UW * q1]
+
     if core == root:
-        g.dma_start(T.y[:, 512 * root_rank:512 * (root_rank + 1)], T.x[:, :]).then_inc(s.stored, 16)
-        n = 1
-        for j0, j1 in COPIES:
-            for j in range(j0, j1 + 1):
-                for q in range(K):
-                    g.wait_ge(arr[j * K + q], engines(hops[j, q][-2], root)[1])
-            g.dma_start(T.y[:, 512 * j0:512 * (j1 + 1)], T.land[:, 512 * j0:512 * (j1 + 1)]).then_inc(s.stored, 16)
-            n += 1
-        g.wait_ge(s.stored, 16 * n)
+        g.dma_start(T.y[:, 512 * root_rank:512 * (root_rank + 1)], T.x[:, :]).then_inc(s.stg, 16)
+        groups = []
+        for j in sorted(ASSIGN):
+            q = 0
+            while q < K:
+                e = q + 1
+                while e < K and e - q < SMAX and ASSIGN[j][e] == ASSIGN[j][q]:
+                    e += 1
+                groups.append((max(est[j, i] for i in range(q, e)), j, q, e))
+                q = e
+        groups.sort()
+        for t, j, q0, q1 in groups:
+            qu = g.sync if ASSIGN[j][q0] in 'AD' else g.scalar
+            for q in range(q0, q1):
+                qu.wait_ge(arr[j * K + q], ne(hops[j, q][-2], root))
+            qu.dma_start(yblock(j, q0, q1), block(j, q0, q1)).then_inc(s.st, 16)
+        g.wait_ge(s.stg, 16)
+        g.wait_ge(s.st, 16 * len(groups))
         return
     work = sorted(((est[u] - LAT * (len(h) - 1 - h.index(core)), u, h.index(core)) for u, h in hops.items() if core in h[:-1]))
     if not work:
         return
     if rank is not None:
         work.sort(key=lambda w: w[1][1])
-        g.dma_start(T.land[:, 512 * rank:512 * (rank + 1)], T.x[:, :]).then_inc(s.ld, 16)
-        g.wait_ge(s.ld, 16)
+        for q in range(K):
+            qu = g.sync if q % 2 == 0 else g.scalar
+            qu.dma_start(block(rank, q, q + 1), xblock(q, q + 1)).then_inc(ld[q], 16)
     sent = 0
     for t, (j, q), k in work:
         h = hops[j, q]
         if k > 0:
-            g.wait_ge(arr[j * K + q], engines(h[k - 1], core)[1])
-        m, ne = engines(core, h[k + 1])
+            g.wait_ge(arr[j * K + q], ne(h[k - 1], core))
+        else:
+            g.wait_ge(ld[q], 16)
         rid, pid, se = topo.addr(h[k + 1])
-        ap = T.land[:, 512 * j + UW * q:512 * j + UW * (q + 1)]
-        g.remote_dma(ap, ap, arr[j * K + q], s.sent, pid, rid, m)
-        sent += ne
+        g.remote_dma(unit(j, q), unit(j, q), arr[j * K + q], s.sent, pid, rid, topo.mask(core, h[k + 1]))
+        sent += ne(core, h[k + 1])
     g.wait_ge(s.sent, sent)

@@ -1,15 +1,16 @@
-MODE = 'dram'
+MODE = 'sbuf'
 K = 4
 UW = 512 // K
 UR = 128 // K
 LAT = 3.0
 SMAX = 2
+LG = 1
 ASSIGN = {0: 'AAAA', 1: 'AAAA', 2: 'BBBB', 4: 'CBBB', 5: 'CCCC', 6: 'DDCC', 7: 'DDDD'}
 if MODE == 'dram':
     SCRATCH = {'land': ('dram', [8 * K, 128, UW], 'float32')}
 else:
     SCRATCH = {'land': ('sbuf', [128, 4096], 'float32')}
-SEMAPHORES = ['sent', 'st', 'stg'] + ['ld%d' % i for i in range(4)] + ['a%d' % i for i in range(32)]
+SEMAPHORES = ['sent', 'st', 'stg'] + ['ld%d' % i for i in range(4)] + ['a%d' % i for i in range(64)]
 
 
 def plan(cores, root_rank):
@@ -46,7 +47,7 @@ def plan(cores, root_rank):
 
 def rank_program(g, core, T, topo):
     s = T.sem
-    arr = [s.a0, s.a1, s.a2, s.a3, s.a4, s.a5, s.a6, s.a7, s.a8, s.a9, s.a10, s.a11, s.a12, s.a13, s.a14, s.a15, s.a16, s.a17, s.a18, s.a19, s.a20, s.a21, s.a22, s.a23, s.a24, s.a25, s.a26, s.a27, s.a28, s.a29, s.a30, s.a31]
+    arr = [s.a0, s.a1, s.a2, s.a3, s.a4, s.a5, s.a6, s.a7, s.a8, s.a9, s.a10, s.a11, s.a12, s.a13, s.a14, s.a15, s.a16, s.a17, s.a18, s.a19, s.a20, s.a21, s.a22, s.a23, s.a24, s.a25, s.a26, s.a27, s.a28, s.a29, s.a30, s.a31, s.a32, s.a33, s.a34, s.a35, s.a36, s.a37, s.a38, s.a39, s.a40, s.a41, s.a42, s.a43, s.a44, s.a45, s.a46, s.a47, s.a48, s.a49, s.a50, s.a51, s.a52, s.a53, s.a54, s.a55, s.a56, s.a57, s.a58, s.a59, s.a60, s.a61, s.a62, s.a63]
     ld = [s.ld0, s.ld1, s.ld2, s.ld3]
     cores = list(T.cores)
     root_rank = T.root if T.root is not None else 3
@@ -102,16 +103,16 @@ def rank_program(g, core, T, topo):
         return
     if rank is not None:
         work.sort(key=lambda w: w[1][1])
-        for q in range(K):
-            qu = g.sync if q % 2 == 0 else g.scalar
-            qu.dma_start(block(rank, q, q + 1), xblock(q, q + 1)).then_inc(ld[q], 16)
+        for i in range(K // LG):
+            qu = g.sync if i % 2 == 0 else g.scalar
+            qu.dma_start(block(rank, LG * i, LG * (i + 1)), xblock(LG * i, LG * (i + 1))).then_inc(ld[i], 16)
     sent = 0
     for t, (j, q), k in work:
         h = hops[j, q]
         if k > 0:
             g.wait_ge(arr[j * K + q], ne(h[k - 1], core))
-        else:
-            g.wait_ge(ld[q], 16)
+        elif q % LG == 0:
+            g.wait_ge(ld[q // LG], 16)
         rid, pid, se = topo.addr(h[k + 1])
         g.remote_dma(unit(j, q), unit(j, q), arr[j * K + q], s.sent, pid, rid, topo.mask(core, h[k + 1]))
         sent += ne(core, h[k + 1])

MODE = 'sbuf'
K = 4
UW = 512 // K
UR = 128 // K
LAT = 3.0
SMAX = 2
LG = 1
ASSIGN = {0: 'AAAA', 1: 'AAAA', 2: 'BBBB', 4: 'CBBB', 5: 'CCCC', 6: 'DDCC', 7: 'DDDD'}
if MODE == 'dram':
    SCRATCH = {'land': ('dram', [8 * K, 128, UW], 'float32')}
else:
    SCRATCH = {'land': ('sbuf', [128, 4096], 'float32')}
SEMAPHORES = ['sent', 'st', 'stg'] + ['ld%d' % i for i in range(4)] + ['a%d' % i for i in range(64)]


def plan(cores, root_rank):
    root = cores[root_rank]
    mate = root // 8 ^ 1
    hops = {}
    est = {}
    for p in 'ABCD':
        lists = [[(j, q) for q in range(K) if ASSIGN[j][q] == p] for j in sorted(ASSIGN)]
        lists = [x for x in lists if x]
        lists.sort(key=lambda x: (x[0][1], -len(x)))
        stream = []
        i = 0
        while any((i < len(x) for x in lists)):
            stream += [x[i] for x in lists if i < len(x)]
            i += 1
        for pos, (j, q) in enumerate(stream):
            src = cores[j]
            base = src // 8 * 8
            alt = pos % 2
            if p == 'A':
                h = [src, root]
            elif p == 'B':
                free = [4, 5] if 'D' in ASSIGN[j] else [4, 5, 6, 7]
                h = [src, base + free[q % len(free)], root]
            elif p == 'C':
                h = [src, mate * 8 + 2 + alt, root]
            else:
                h = [src, base + 6 + q % 2, mate * 8 + 6 + alt, root]
            hops[j, q] = h
            est[j, q] = LAT * (len(h) - 1) + pos + 1
    return (hops, est)


def rank_program(g, core, T, topo):
    s = T.sem
    arr = [s.a0, s.a1, s.a2, s.a3, s.a4, s.a5, s.a6, s.a7, s.a8, s.a9, s.a10, s.a11, s.a12, s.a13, s.a14, s.a15, s.a16, s.a17, s.a18, s.a19, s.a20, s.a21, s.a22, s.a23, s.a24, s.a25, s.a26, s.a27, s.a28, s.a29, s.a30, s.a31, s.a32, s.a33, s.a34, s.a35, s.a36, s.a37, s.a38, s.a39, s.a40, s.a41, s.a42, s.a43, s.a44, s.a45, s.a46, s.a47, s.a48, s.a49, s.a50, s.a51, s.a52, s.a53, s.a54, s.a55, s.a56, s.a57, s.a58, s.a59, s.a60, s.a61, s.a62, s.a63]
    ld = [s.ld0, s.ld1, s.ld2, s.ld3]
    cores = list(T.cores)
    root_rank = T.root if T.root is not None else 3
    root = cores[root_rank]
    hops, est = plan(cores, root_rank)
    rank = T.rank_of(core)

    def ne(a, b):
        return bin(topo.mask(a, b)).count('1')

    def unit(j, q):
        if MODE == 'dram':
            return T.land[j * K + q]
        return T.land[:, 512 * j + UW * q:512 * j + UW * (q + 1)]

    def block(j, q0, q1):
        if MODE == 'dram':
            return T.land[j * K + q0:j * K + q1]
        return T.land[:, 512 * j + UW * q0:512 * j + UW * q1]

    def xblock(q0, q1):
        if MODE == 'dram':
            return T.x[UR * q0:UR * q1, :]
        return T.x[:, UW * q0:UW * q1]

    def yblock(j, q0, q1):
        if MODE == 'dram':
            return T.y[UR * q0:UR * q1, 512 * j:512 * (j + 1)]
        return T.y[:, 512 * j + UW * q0:512 * j + UW * q1]

    if core == root:
        g.dma_start(T.y[:, 512 * root_rank:512 * (root_rank + 1)], T.x[:, :]).then_inc(s.stg, 16)
        groups = []
        for j in sorted(ASSIGN):
            q = 0
            while q < K:
                e = q + 1
                while e < K and e - q < SMAX and ASSIGN[j][e] == ASSIGN[j][q]:
                    e += 1
                groups.append((max(est[j, i] for i in range(q, e)), j, q, e))
                q = e
        groups.sort()
        for t, j, q0, q1 in groups:
            qu = g.sync if ASSIGN[j][q0] in 'AD' else g.scalar
            for q in range(q0, q1):
                qu.wait_ge(arr[j * K + q], ne(hops[j, q][-2], root))
            qu.dma_start(yblock(j, q0, q1), block(j, q0, q1)).then_inc(s.st, 16)
        g.wait_ge(s.stg, 16)
        g.wait_ge(s.st, 16 * len(groups))
        return
    work = sorted(((est[u] - LAT * (len(h) - 1 - h.index(core)), u, h.index(core)) for u, h in hops.items() if core in h[:-1]))
    if not work:
        return
    if rank is not None:
        work.sort(key=lambda w: w[1][1])
        for i in range(K // LG):
            qu = g.sync if i % 2 == 0 else g.scalar
            qu.dma_start(block(rank, LG * i, LG * (i + 1)), xblock(LG * i, LG * (i + 1))).then_inc(ld[i], 16)
    sent = 0
    for t, (j, q), k in work:
        h = hops[j, q]
        if k > 0:
            g.wait_ge(arr[j * K + q], ne(h[k - 1], core))
        elif q % LG == 0:
            g.wait_ge(ld[q // LG], 16)
        rid, pid, se = topo.addr(h[k + 1])
        g.remote_dma(unit(j, q), unit(j, q), arr[j * K + q], s.sent, pid, rid, topo.mask(core, h[k + 1]))
        sent += ne(core, h[k + 1])
    g.wait_ge(s.sent, sent)
